import numpy as np
import ml_dtypes


def mxq(x, axis, fmt="e4m3"):
    dtype, down = {"e4m3": (ml_dtypes.float8_e4m3fn, 7), "e5m2": (ml_dtypes.float8_e5m2, 14)}[fmt]
    v = np.moveaxis(np.asarray(x, np.float32).astype(ml_dtypes.bfloat16).astype(np.float64), axis, -1)
    blocks = v.reshape(v.shape[:-1] + (-1, 32))
    amax = np.abs(blocks).max(-1, keepdims=True)
    byte = np.maximum(np.where(amax > 0, np.frexp(amax)[1] - 1 + 127, 0) - down, 1)
    scale = np.exp2(byte - 127.0)
    codes = (blocks / scale).astype(np.float32).astype(dtype).astype(np.float64)
    return np.moveaxis((codes * scale).reshape(v.shape), -1, axis)


WIDE = False


def mx_kscale(k):
    if not WIDE:
        return np.ones(k)
    levels = np.array([10, -10, 5, -5, 0])
    if k % 512:
        return np.exp2(np.random.permutation(np.resize(levels, k // 32))).repeat(32)
    a = np.empty((k // 512, 16))
    for p in range(k // 512):
        a[p, :8] = np.random.permutation(np.resize(levels, 8))
        for g in range(8):
            far = levels[np.abs(levels - a[p, g]) >= 10]
            a[p, g + 8] = far[np.random.randint(len(far))]
    return np.exp2(a.ravel()).repeat(32)


def f64(x):
    return np.asarray(x).astype(np.float64)


def striped(idx):
    return np.tile(idx.reshape(-1, 16).T, (8, 1)).astype(np.uint16)


def unstriped(offs):
    return offs[:16].T.reshape(-1).astype(np.int64)


def striped8(idx):
    return np.concatenate([x.reshape(-1, 16).T for x in idx]).astype(np.uint16)


def runs(offs, k):
    lists = np.stack([offs[16 * r : 16 * r + 16].T.reshape(-1) for r in range(8)]).astype(np.int64)
    return lists[np.arange(k) % 512 // 64]


def pack_weight(w):
    k, n = w.shape
    w = f64(np.asarray(w, np.float32).astype(ml_dtypes.bfloat16)).reshape(k // 32, 32, n)
    amax = np.abs(w).max(1)
    byte = np.clip(np.where(amax > 0, np.frexp(amax)[1] - 1 + 127 - 7, 1), 1, 254)
    scaled = (w * np.exp2(127.0 - byte)[:, None, :]).reshape(k, n).astype(np.float32)
    words = np.ascontiguousarray(scaled.reshape(k // 512, 128, 4, n).transpose(0, 1, 3, 2)).astype(ml_dtypes.float8_e4m3fn).view(np.uint8)
    return words, np.ascontiguousarray(byte.astype(np.uint8).reshape(k // 512, 16, n))


def unpack_weight(words, scales):
    g, p, n, _ = words.shape
    vals = np.ascontiguousarray(words).view(ml_dtypes.float8_e4m3fn).astype(np.float64) * np.repeat(np.exp2(scales.astype(np.float64) - 127.0), 8, axis=1)[..., None]
    return vals.transpose(0, 1, 3, 2).reshape(g * 512, n)


E2M1 = np.array([0.0, 0.5, 1.0, 1.5, 2.0, 3.0, 4.0, 6.0, -0.0, -0.5, -1.0, -1.5, -2.0, -3.0, -4.0, -6.0])


def pack_fp4(w):
    k, n = w.shape
    w = f64(np.asarray(w, np.float32).astype(ml_dtypes.bfloat16)).reshape(k // 32, 32, n)
    amax = np.abs(w).max(1)
    mant, ex = np.frexp(amax / 6.0)
    byte = np.clip(np.where(amax > 0, np.where(mant > 0.5, ex, ex - 1) + 127, 1), 1, 254)
    scaled = (w * np.exp2(127.0 - byte)[:, None, :]).reshape(k, n).astype(np.float32)
    c = np.ascontiguousarray(scaled.reshape(k // 512, 128, 4, n).transpose(0, 1, 3, 2)).astype(ml_dtypes.float4_e2m1fn).view(np.uint8) & 0xF
    words = (c[..., 0::2] | (c[..., 1::2] << 4)).reshape(k // 512, 128, 2 * n)
    return np.ascontiguousarray(words), np.ascontiguousarray(byte.astype(np.uint8).reshape(k // 512, 16, n))


def unpack_fp4(words, scales):
    g, _, n = scales.shape
    words = np.ascontiguousarray(words).reshape(g, 128, n, 2)
    nib = np.empty((g, 128, n, 4), np.uint8)
    nib[..., 0::2] = words & 0xF
    nib[..., 1::2] = words >> 4
    vals = E2M1[nib] * np.repeat(np.exp2(scales.astype(np.float64) - 127.0), 8, axis=1)[..., None]
    return vals.transpose(0, 1, 3, 2).reshape(g * 512, n)


def planes(y):
    n, m = y.shape
    v = y.astype(np.float32).astype(ml_dtypes.bfloat16).astype(np.float64).reshape(n // 32, 32, m)
    top = np.abs(v).max(1)
    byte = np.clip(np.where(top > 0, np.frexp(top)[1] - 1 + 127 - 7, 1), 1, 254)
    codes = (v * np.exp2(127.0 - byte)[:, None, :]).reshape(n, m).astype(np.float32).astype(ml_dtypes.float8_e4m3fn).view(np.uint8)
    words = codes.reshape(n // 512, 128, 4, m).transpose(0, 1, 3, 2)
    return np.ascontiguousarray(words), np.ascontiguousarray(byte.astype(np.uint8).reshape(n // 512, 16, m))


K, T, S, N, H = 512, 2048, 512, 512, 512


def setup_inputs():
    n = np.random.standard_normal
    s = mx_kscale(K)[:, None]
    u = mx_kscale(H)
    packed_xT = pack_weight(n((K, T)) * s)
    packed_w1 = pack_fp4(n((K, H)) / np.sqrt(K) / s)
    packed_w2 = pack_fp4(n((H, N)) / np.sqrt(H) / u[:, None])
    return {
        "x_words": packed_xT[0],
        "x_scales": packed_xT[1],
        "w1_words": packed_w1[0],
        "w1_scales": packed_w1[1],
        "rec": (0.3 * n((H, S))).astype(np.float32),
        "gn": (np.random.uniform(0.5, 1.5, (H, 1)) * u[:, None]).astype(np.float32),
        "w2_words": packed_w2[0],
        "w2_scales": packed_w2[1],
        "offs": striped(np.random.permutation(T)[:S]),
        "west": striped8(np.stack([np.random.permutation(S) for _ in range(8)])),
        "east": striped8(np.stack([np.random.permutation(S) for _ in range(8)])),
    }


def reference(x_words, x_scales, w1_words, w1_scales, rec, gn, w2_words, w2_scales, offs, west, east):
    xq = unpack_weight(x_words, x_scales)[:, unstriped(offs)]
    y = np.tanh(unpack_fp4(w1_words, w1_scales).T @ xq)
    z = f64(gn) * (1.5 * y - (0.3125 * (y * ((y) ** 2))) - f64(rec) + 0.25 * (y[np.arange(H)[:, None], runs(west, H)] + y[np.arange(H)[:, None], runs(east, H)] - (2.0 * y)))
    out_0 = unpack_fp4(w2_words, w2_scales).T @ mxq(z, 0, "e4m3")
    return (out_0,) + planes(out_0)

@@ -1,0 +1,223 @@
+import math
+from contextlib import ExitStack
+
+import concourse.mybir as mybir
+
+K, T, S, N, H = 512, 2048, 512, 512, 512
+FLOPS = 2 * K * H * S + 2 * H * N * S
+
+F32 = mybir.dt.float32
+BF16 = mybir.dt.bfloat16
+I32 = mybir.dt.int32
+U32 = mybir.dt.uint32
+U16 = mybir.dt.uint16
+U8 = mybir.dt.uint8
+FP8X4 = mybir.dt.float8_e4m3fn_x4
+FP4X4 = mybir.dt.float4_e2m1fn_x4
+ACT = mybir.ActivationFunctionType
+ALU = mybir.AluOpType
+
+P = 128
+PACK = 4
+HALF = S // 2
+CHUNKS = [(0, 256), (256, 128), (384, 128)]
+
+
+def tile_picked_fhn8_none_po_kernel(
+    tc, x_words, x_scales, w1_words, w1_scales, rec, gn, w2_words, w2_scales, offs, west, east, out_0, out_1, out_2
+):
+    nc = tc.nc
+    with ExitStack() as ctx:
+        keep = ctx.enter_context(tc.tile_pool(name="keep", bufs=1))
+        psum = ctx.enter_context(tc.psum_pool(name="psum", bufs=1))
+
+        def load_scales(queues, tile, rows):
+            for q, queue in enumerate(queues):
+                queue.dma_start(tile[32 * q : 32 * q + 4, :].bitcast(I32), rows[0, 4 * q : 4 * q + 4, :].bitcast(I32))
+
+        def deal_words(raw, dealt):
+            nc.vector.tensor_copy(
+                dealt[:].bitcast(U16).rearrange("p (t m) -> p t m", t=PACK),
+                raw[:].bitcast(U16).rearrange("p (m t) -> p t m", t=PACK),
+            )
+
+        def deal_scales(raw, dealt):
+            nc.vector.tensor_copy(
+                dealt[:].rearrange("p (t m) -> p t m", t=PACK),
+                raw[:].rearrange("p (m t) -> p t m", t=PACK),
+            )
+
+        offs_t = keep.tile([P, S // 16], U16, name="offs_t")
+        west_t = keep.tile([P, S // 16], U16, name="west_t")
+        east_t = keep.tile([P, S // 16], U16, name="east_t")
+        xs = keep.tile([P, T], U8, name="xs", tag="stage_b", align_bytes=64)
+        xw = keep.tile([P, T], U32, name="xw", tag="stage_c", align_bytes=64)
+        w1w_raw = keep.tile([P, 2 * H], U8, name="w1w_raw", tag="stage_a", align_bytes=64)
+        w1s_raw = keep.tile([P, H], U8, name="w1s_raw", tag="stage_d", align_bytes=64)
+        w2w = keep.tile([P, 2 * N], U8, name="w2w", align_bytes=64)
+        w2s = keep.tile([P, N], U8, name="w2s", align_bytes=64)
+        gain = keep.tile([P, PACK], F32, name="gain")
+        quarter = keep.tile([P, PACK], F32, name="quarter")
+        warm = keep.tile([P, 1], F32, name="warm")
+        warm_out = keep.tile([P, 1], F32, name="warm_out")
+
+        nc.vector.memset(xs[:].bitcast(I32), 0)
+        nc.gpsimd.memset(w1s_raw[:].bitcast(I32), 0)
+        nc.vector.memset(warm[:], 0.0)
+
+        nc.sync.dma_start(offs_t[:], offs)
+        nc.sync.dma_start(west_t[:], west)
+        nc.sync.dma_start(east_t[:], east)
+        nc.sync.dma_start(xw[:].bitcast(I32), x_words[0].rearrange("p c r -> p (c r)").bitcast(I32))
+        nc.gpsimd.dma_start(w1w_raw[:].bitcast(I32), w1_words[0].bitcast(I32))
+        load_scales([nc.scalar] * 4, xs, x_scales)
+        load_scales([nc.scalar, nc.scalar, nc.scalar, nc.gpsimd], w1s_raw, w1_scales)
+        nc.gpsimd.dma_start(gain[:], gn.rearrange("(p t) o -> p (t o)", t=PACK))
+        nc.scalar.activation(warm_out[:], warm[:], ACT.Tanh)
+        nc.gpsimd.tensor_scalar(quarter[:], gain[:], 0.25, 0.0, ALU.mult, ALU.add)
+        rec_rows = rec.rearrange("(p t) j -> p t j", t=PACK)
+
+        xg_s = keep.tile([P, S], U8, name="xg_s", tag="stage_e", align_bytes=64)
+        xg_w = [keep.tile([P, HALF], U32, name="xg_w%d" % h, tag="stage_f%d" % h, align_bytes=64) for h in range(2)]
+        nc.vector.tensor_copy(xg_s[:], xs[:].indirect(offs_t[:]))
+        w1w = keep.tile([P, 2 * H], U8, name="w1w", tag="stage_b", align_bytes=64)
+        deal_words(w1w_raw, w1w)
+        w1s = keep.tile([P, H], U8, name="w1s", tag="stage_a", align_bytes=64)
+        deal_scales(w1s_raw, w1s)
+        rec0 = keep.tile([P, PACK, HALF], F32, name="rec0", tag="stage_d", align_bytes=64)
+        nc.sync.dma_start(rec0[:], rec_rows[:, :, 0:HALF])
+        for h in range(2):
+            nc.vector.tensor_copy(xg_w[h][:], xw[:].indirect(offs_t[:, h * HALF // 16 : (h + 1) * HALF // 16]))
+        w2w_raw = keep.tile([P, 2 * N], U8, name="w2w_raw", tag="stage_c", align_bytes=64)
+        nc.sync.dma_start(w2w_raw[:].bitcast(I32), w2_words[0].bitcast(I32))
+
+        y = [keep.tile([P, S], F32, name="y%d" % t) for t in range(PACK)]
+        sq = [[keep.tile([P, HALF], F32, name="sq%d_%d" % (t, h)) for h in range(2)] for t in range(PACK)]
+        rg = [[keep.tile([P, HALF], F32, name="rg%d_%d" % (t, h)) for h in range(2)] for t in range(PACK)]
+        acc = {}
+        for h in range(2):
+            for t in range(PACK):
+                if t == 0:
+                    acc[(t, h)] = psum.tile([P, HALF], F32, name="acc0_%d" % h, tag="bank%d" % h)[:]
+                elif h == 0:
+                    whole = psum.tile([P, S], F32, name="acc%d" % t, tag="bank%d" % (t + 1))
+                    acc[(t, 0)] = whole[:, 0:HALF]
+                    acc[(t, 1)] = whole[:, HALF:S]
+                    acc[(t, 2)] = whole[:]
+                nc.tensor.matmul_mx(
+                    acc[(t, h)],
+                    lhsT=w1w[:, 2 * P * t : 2 * P * (t + 1)].bitcast(FP4X4),
+                    lhsT_scale=w1s[:, P * t : P * (t + 1)],
+                    rhs=xg_w[h][:].bitcast(FP8X4),
+                    rhs_scale=xg_s[:, h * HALF : (h + 1) * HALF],
+                    start=True,
+                    stop=True,
+                )
+        alpha = math.sqrt(1.25)
+        rec1 = keep.tile([P, PACK, HALF], F32, name="rec1", tag="stage_e", align_bytes=64)
+        nc.sync.dma_start(rec1[:], rec_rows[:, :, HALF:S])
+        rec_t = [rec0, rec1]
+        w2s_raw = keep.tile([P, N], U8, name="w2s_raw", tag="stage_f0", align_bytes=64)
+        nc.gpsimd.memset(w2s_raw[:].bitcast(I32), 0)
+        load_scales([nc.sync] * 4, w2s_raw, w2_scales)
+
+        def square(t, h):
+            nc.scalar.activation(sq[t][h][:], y[t][:, h * HALF : (h + 1) * HALF], ACT.Square, scale=alpha)
+
+        def scale_rec(t, h):
+            nc.scalar.activation(rg[t][h][:], rec_t[h][:, t, :], ACT.Copy, scale=gain[:, t : t + 1])
+
+        for t in range(PACK):
+            if t == 0:
+                nc.scalar.activation(y[0][:, 0:HALF], acc[(0, 0)], ACT.Tanh)
+                square(0, 0)
+                nc.scalar.activation(y[0][:, HALF:S], acc[(0, 1)], ACT.Tanh)
+            else:
+                nc.scalar.activation(y[t][:], acc[(t, 2)], ACT.Tanh)
+                square(t, 0)
+            scale_rec(t, 0)
+        for t in range(PACK):
+            square(t, 1)
+            scale_rec(t, 1)
+
+        ow = keep.tile([P, S], U32, name="ow", align_bytes=64)
+        osc = keep.tile([P, S], U8, name="osc", align_bytes=64)
+        out_rows = out_0.rearrange("(p t) j -> p t j", t=PACK)
+        out_words = out_1[0].rearrange("p c r -> p (c r)").bitcast(I32)
+
+        def front(ci):
+            c0, w = CHUNKS[ci]
+            h, o = divmod(c0, HALF)
+            lists = slice(c0 // 16, (c0 + w) // 16)
+            zb = keep.tile([P, PACK, w], BF16, name="zb%d" % ci)
+            cub = [keep.tile([P, w], F32, name="cub%d_%d" % (ci, t)) for t in range(PACK)]
+            g1 = [keep.tile([P, w], F32, name="g1%d_%d" % (ci, t)) for t in range(PACK)]
+            g2 = [keep.tile([P, w], F32, name="g2%d_%d" % (ci, t)) for t in range(PACK)]
+
+            def step(k, t):
+                if k == 0:
+                    nc.vector.scalar_tensor_tensor(cub[t][:], sq[t][h][:, o : o + w], 4.0, y[t][:, c0 : c0 + w], ALU.subtract, ALU.mult)
+                elif k == 1:
+                    nc.vector.tensor_tensor(g1[t][:], y[t][:].indirect(west_t[:, lists]), cub[t][:], ALU.subtract)
+                elif k == 2:
+                    nc.vector.tensor_tensor(g2[t][:], y[t][:].indirect(east_t[:, lists]), g1[t][:], ALU.add)
+                else:
+                    nc.vector.scalar_tensor_tensor(zb[:, t, :], g2[t][:], quarter[:, t : t + 1], rg[t][h][:, o : o + w], ALU.mult, ALU.subtract)
+
+            for pair in range(2):
+                for k in range(4):
+                    for t in (2 * pair, 2 * pair + 1):
+                        step(k, t)
+            return zb
+
+        def back(ci, zb):
+            c0, w = CHUNKS[ci]
+            last = ci == len(CHUNKS) - 1
+            zi = keep.tile([P, w, PACK], BF16, name="zi%d" % ci, align_bytes=64)
+            if last:
+                nc.vector.tensor_copy(zi[:], zb[:].rearrange("p t c -> p c t"))
+            else:
+                nc.scalar.copy(zi[:], zb[:].rearrange("p t c -> p c t"))
+            zw = keep.tile([P, w], U32, name="zw%d" % ci, align_bytes=64)
+            zs = keep.tile([P, w], U8, name="zs%d" % ci, align_bytes=64)
+            nc.vector.quantize_mx(zw[:].bitcast(FP8X4), zs[:], zi[:].rearrange("p c t -> p (c t)"))
+            per_bank = S // w
+            staged = keep.tile([P, PACK, w], F32, name="staged%d" % ci)
+            banks = []
+            for b in range(PACK // per_bank):
+                bank = psum.tile([P, per_bank, w], F32, name="o%d_%d" % (ci, b), tag="bank%d" % ((5 + 2 * ci + b) % 8))
+                banks.append(bank)
+                for u in range(per_bank):
+                    t = b * per_bank + u
+                    nc.tensor.matmul_mx(
+                        bank[:, u, :],
+                        lhsT=w2w[:, 2 * P * t : 2 * P * (t + 1)].bitcast(FP4X4),
+                        lhsT_scale=w2s[:, P * t : P * (t + 1)],
+                        rhs=zw[:].bitcast(FP8X4),
+                        rhs_scale=zs[:],
+                        start=True,
+                        stop=True,
+                    )
+                nc.scalar.copy(staged[:, b * per_bank : (b + 1) * per_bank, :], bank[:])
+            nc.sync.dma_start(out_rows[:, :, c0 : c0 + w], staged[:])
+            oi = keep.tile([P, w, PACK], BF16, name="oi%d" % ci, align_bytes=64)
+            if last:
+                nc.vector.tensor_copy(oi[:], staged[:].rearrange("p t c -> p c t"))
+            else:
+                nc.scalar.copy(oi[:], staged[:].rearrange("p t c -> p c t"))
+            return oi
+
+        def finish(ci, oi):
+            c0, w = CHUNKS[ci]
+            nc.vector.quantize_mx(ow[:, c0 : c0 + w].bitcast(FP8X4), osc[:, c0 : c0 + w], oi[:].rearrange("p c t -> p (c t)"))
+            nc.sync.dma_start(out_words[:, c0 : c0 + w], ow[:, c0 : c0 + w].bitcast(I32))
+
+        for ci in range(len(CHUNKS)):
+            zb = front(ci)
+            if ci == 0:
+                deal_words(w2w_raw, w2w)
+                deal_scales(w2s_raw, w2s)
+            finish(ci, back(ci, zb))
+        for q in range(4):
+            queue = nc.scalar if q % 2 else nc.sync
+            queue.dma_start(out_2[0, 4 * q : 4 * q + 4, :].bitcast(I32), osc[32 * q : 32 * q + 4, :].bitcast(I32))

@@ -51,75 +51,72 @@ def tile_picked_fhn8_none_po_kernel(
         west_t = keep.tile([P, S // 16], U16, name="west_t")
         east_t = keep.tile([P, S // 16], U16, name="east_t")
         xs = keep.tile([P, T], U8, name="xs", tag="stage_b", align_bytes=64)
-        xw = keep.tile([P, T], U32, name="xw", tag="stage_c", align_bytes=64)
+        zeros = keep.tile([P, H], U8, name="zeros", tag="stage_c", align_bytes=64)
         w1w_raw = keep.tile([P, 2 * H], U8, name="w1w_raw", tag="stage_a", align_bytes=64)
         w1s_raw = keep.tile([P, H], U8, name="w1s_raw", tag="stage_d", align_bytes=64)
         w2w = keep.tile([P, 2 * N], U8, name="w2w", align_bytes=64)
-        w2s = keep.tile([P, N], U8, name="w2s", align_bytes=64)
         gain = keep.tile([P, PACK], F32, name="gain")
         quarter = keep.tile([P, PACK], F32, name="quarter")
-        warm = keep.tile([P, 1], F32, name="warm")
-        warm_out = keep.tile([P, 1], F32, name="warm_out")
 
         nc.vector.memset(xs[:].bitcast(I32), 0)
-        nc.gpsimd.memset(w1s_raw[:].bitcast(I32), 0)
-        nc.vector.memset(warm[:], 0.0)
+        nc.vector.memset(zeros[:].bitcast(I32), 0)
+        nc.vector.tensor_copy(w1s_raw[:].bitcast(I32), zeros[:].bitcast(I32))
+        xw = keep.tile([P, T], U32, name="xw", tag="stage_c", align_bytes=64)
 
         nc.sync.dma_start(offs_t[:], offs)
+        nc.gpsimd.dma_start(w1w_raw[:].bitcast(I32), w1_words[0].bitcast(I32))
+        load_scales([nc.sync, nc.sync, nc.scalar, nc.scalar], xs, x_scales)
+        nc.scalar.dma_start(xw[:].bitcast(I32), x_words[0].rearrange("p c r -> p (c r)").bitcast(I32))
+        load_scales([nc.scalar] * 4, w1s_raw, w1_scales)
         nc.sync.dma_start(west_t[:], west)
         nc.sync.dma_start(east_t[:], east)
-        nc.sync.dma_start(xw[:].bitcast(I32), x_words[0].rearrange("p c r -> p (c r)").bitcast(I32))
-        nc.gpsimd.dma_start(w1w_raw[:].bitcast(I32), w1_words[0].bitcast(I32))
-        load_scales([nc.scalar] * 4, xs, x_scales)
-        load_scales([nc.scalar, nc.scalar, nc.scalar, nc.gpsimd], w1s_raw, w1_scales)
         nc.gpsimd.dma_start(gain[:], gn.rearrange("(p t) o -> p (t o)", t=PACK))
-        nc.scalar.activation(warm_out[:], warm[:], ACT.Tanh)
         nc.gpsimd.tensor_scalar(quarter[:], gain[:], 0.25, 0.0, ALU.mult, ALU.add)
         rec_rows = rec.rearrange("(p t) j -> p t j", t=PACK)
 
         xg_s = keep.tile([P, S], U8, name="xg_s", tag="stage_e", align_bytes=64)
-        xg_w = [keep.tile([P, HALF], U32, name="xg_w%d" % h, tag="stage_f%d" % h, align_bytes=64) for h in range(2)]
         nc.vector.tensor_copy(xg_s[:], xs[:].indirect(offs_t[:]))
-        w1w = keep.tile([P, 2 * H], U8, name="w1w", tag="stage_b", align_bytes=64)
-        deal_words(w1w_raw, w1w)
-        w1s = keep.tile([P, H], U8, name="w1s", tag="stage_a", align_bytes=64)
-        deal_scales(w1s_raw, w1s)
-        rec0 = keep.tile([P, PACK, HALF], F32, name="rec0", tag="stage_d", align_bytes=64)
+        rec0 = keep.tile([P, PACK, HALF], F32, name="rec0", tag="stage_b", align_bytes=64)
         nc.sync.dma_start(rec0[:], rec_rows[:, :, 0:HALF])
-        for h in range(2):
-            nc.vector.tensor_copy(xg_w[h][:], xw[:].indirect(offs_t[:, h * HALF // 16 : (h + 1) * HALF // 16]))
+        w1w = keep.tile([P, 2 * H], U8, name="w1w", align_bytes=64)
+        w1s = keep.tile([P, H], U8, name="w1s", align_bytes=64)
+        deal_words(w1w_raw, w1w)
+        xg_w0 = keep.tile([P, HALF], U32, name="xg_w0", tag="stage_a", align_bytes=64)
+        nc.vector.tensor_copy(xg_w0[:], xw[:].indirect(offs_t[:, 0 : HALF // 16]))
+        deal_scales(w1s_raw, w1s)
+        xg_w1 = keep.tile([P, HALF], U32, name="xg_w1", tag="stage_d", align_bytes=64)
+        nc.vector.tensor_copy(xg_w1[:], xw[:].indirect(offs_t[:, HALF // 16 : S // 16]))
+        xg_w = [xg_w0, xg_w1]
         w2w_raw = keep.tile([P, 2 * N], U8, name="w2w_raw", tag="stage_c", align_bytes=64)
         nc.sync.dma_start(w2w_raw[:].bitcast(I32), w2_words[0].bitcast(I32))
-
         y = [keep.tile([P, S], F32, name="y%d" % t) for t in range(PACK)]
         sq = [[keep.tile([P, HALF], F32, name="sq%d_%d" % (t, h)) for h in range(2)] for t in range(PACK)]
         rg = [[keep.tile([P, HALF], F32, name="rg%d_%d" % (t, h)) for h in range(2)] for t in range(PACK)]
-        acc = {}
-        for h in range(2):
-            for t in range(PACK):
-                if t == 0:
-                    acc[(t, h)] = psum.tile([P, HALF], F32, name="acc0_%d" % h, tag="bank%d" % h)[:]
-                elif h == 0:
-                    whole = psum.tile([P, S], F32, name="acc%d" % t, tag="bank%d" % (t + 1))
-                    acc[(t, 0)] = whole[:, 0:HALF]
-                    acc[(t, 1)] = whole[:, HALF:S]
-                    acc[(t, 2)] = whole[:]
-                nc.tensor.matmul_mx(
-                    acc[(t, h)],
-                    lhsT=w1w[:, 2 * P * t : 2 * P * (t + 1)].bitcast(FP4X4),
-                    lhsT_scale=w1s[:, P * t : P * (t + 1)],
-                    rhs=xg_w[h][:].bitcast(FP8X4),
-                    rhs_scale=xg_s[:, h * HALF : (h + 1) * HALF],
-                    start=True,
-                    stop=True,
-                )
+        cub = [[keep.tile([P, HALF], F32, name="cub%d_%d" % (t, h)) for h in range(2)] for t in range(PACK)]
+        def first_product(acc, t, h):
+            nc.tensor.matmul_mx(
+                acc,
+                lhsT=w1w[:, 2 * P * t : 2 * P * (t + 1)].bitcast(FP4X4),
+                lhsT_scale=w1s[:, P * t : P * (t + 1)],
+                rhs=xg_w[h][:].bitcast(FP8X4),
+                rhs_scale=xg_s[:, h * HALF : (h + 1) * HALF],
+                start=True,
+                stop=True,
+            )
+
+        acc0 = [psum.tile([P, HALF], F32, name="acc0_%d" % h, tag="bank%d" % h) for h in range(2)]
+        acc = [None] + [psum.tile([P, S], F32, name="acc%d" % t, tag="bank%d" % (t + 1)) for t in range(1, PACK)]
+        for t in range(PACK):
+            for h in range(2):
+                first_product(acc0[h][:] if t == 0 else acc[t][:, h * HALF : (h + 1) * HALF], t, h)
         alpha = math.sqrt(1.25)
         rec1 = keep.tile([P, PACK, HALF], F32, name="rec1", tag="stage_e", align_bytes=64)
         nc.sync.dma_start(rec1[:], rec_rows[:, :, HALF:S])
         rec_t = [rec0, rec1]
-        w2s_raw = keep.tile([P, N], U8, name="w2s_raw", tag="stage_f0", align_bytes=64)
+        w2s_raw = keep.tile([P, N], U8, name="w2s_raw", tag="stage_a", align_bytes=64)
         nc.gpsimd.memset(w2s_raw[:].bitcast(I32), 0)
         load_scales([nc.sync] * 4, w2s_raw, w2_scales)
+        w2s = keep.tile([P, N], U8, name="w2s", align_bytes=64)
 
         def square(t, h):
             nc.scalar.activation(sq[t][h][:], y[t][:, h * HALF : (h + 1) * HALF], ACT.Square, scale=alpha)
@@ -129,11 +126,11 @@ def tile_picked_fhn8_none_po_kernel(
 
         for t in range(PACK):
             if t == 0:
-                nc.scalar.activation(y[0][:, 0:HALF], acc[(0, 0)], ACT.Tanh)
+                nc.scalar.activation(y[0][:, 0:HALF], acc0[0][:], ACT.Tanh)
                 square(0, 0)
-                nc.scalar.activation(y[0][:, HALF:S], acc[(0, 1)], ACT.Tanh)
+                nc.scalar.activation(y[0][:, HALF:S], acc0[1][:], ACT.Tanh)
             else:
-                nc.scalar.activation(y[t][:], acc[(t, 2)], ACT.Tanh)
+                nc.scalar.activation(y[t][:], acc[t][:], ACT.Tanh)
                 square(t, 0)
             scale_rec(t, 0)
         for t in range(PACK):
@@ -150,15 +147,15 @@ def tile_picked_fhn8_none_po_kernel(
             h, o = divmod(c0, HALF)
             lists = slice(c0 // 16, (c0 + w) // 16)
             zb = keep.tile([P, PACK, w], BF16, name="zb%d" % ci)
-            cub = [keep.tile([P, w], F32, name="cub%d_%d" % (ci, t)) for t in range(PACK)]
             g1 = [keep.tile([P, w], F32, name="g1%d_%d" % (ci, t)) for t in range(PACK)]
             g2 = [keep.tile([P, w], F32, name="g2%d_%d" % (ci, t)) for t in range(PACK)]
 
             def step(k, t):
                 if k == 0:
-                    nc.vector.scalar_tensor_tensor(cub[t][:], sq[t][h][:, o : o + w], 4.0, y[t][:, c0 : c0 + w], ALU.subtract, ALU.mult)
+                    if o == 0:
+                        nc.vector.scalar_tensor_tensor(cub[t][h][:], sq[t][h][:], 4.0, y[t][:, c0 : c0 + HALF], ALU.subtract, ALU.mult)
                 elif k == 1:
-                    nc.vector.tensor_tensor(g1[t][:], y[t][:].indirect(west_t[:, lists]), cub[t][:], ALU.subtract)
+                    nc.vector.tensor_tensor(g1[t][:], y[t][:].indirect(west_t[:, lists]), cub[t][h][:, o : o + w], ALU.subtract)
                 elif k == 2:
                     nc.vector.tensor_tensor(g2[t][:], y[t][:].indirect(east_t[:, lists]), g1[t][:], ALU.add)
                 else:
@@ -212,12 +209,15 @@ def tile_picked_fhn8_none_po_kernel(
             nc.vector.quantize_mx(ow[:, c0 : c0 + w].bitcast(FP8X4), osc[:, c0 : c0 + w], oi[:].rearrange("p c t -> p (c t)"))
             nc.sync.dma_start(out_words[:, c0 : c0 + w], ow[:, c0 : c0 + w].bitcast(I32))
 
+        oi = []
         for ci in range(len(CHUNKS)):
             zb = front(ci)
             if ci == 0:
                 deal_words(w2w_raw, w2w)
                 deal_scales(w2s_raw, w2s)
-            finish(ci, back(ci, zb))
+            oi.append(back(ci, zb))
+        for ci in range(len(CHUNKS)):
+            finish(ci, oi[ci])
         for q in range(4):
             queue = nc.scalar if q % 2 else nc.sync
             queue.dma_start(out_2[0, 4 * q : 4 * q + 4, :].bitcast(I32), osc[32 * q : 32 * q + 4, :].bitcast(I32))

@@ -19,8 +19,13 @@ ALU = mybir.AluOpType
 
 P = 128
 PACK = 4
+GROUP = 16
+QUADRANTS = 4
+BANK = 512
 HALF = S // 2
 CHUNKS = [(0, 256), (256, 128), (384, 128)]
+LAST = len(CHUNKS) - 1
+SECOND_BANKS = [(5, 6), (7,), (1,)]
 
 
 def tile_picked_fhn8_none_po_kernel(
@@ -37,187 +42,206 @@ def tile_picked_fhn8_none_po_kernel(
 
         def deal_words(raw, dealt):
             nc.vector.tensor_copy(
-                dealt[:].bitcast(U16).rearrange("p (t m) -> p t m", t=PACK),
+                dealt.bitcast(U16).rearrange("p (t m) -> p t m", t=PACK),
                 raw[:].bitcast(U16).rearrange("p (m t) -> p t m", t=PACK),
             )
 
         def deal_scales(raw, dealt):
             nc.vector.tensor_copy(
-                dealt[:].rearrange("p (t m) -> p t m", t=PACK),
+                dealt.rearrange("p (t m) -> p t m", t=PACK),
                 raw[:].rearrange("p (m t) -> p t m", t=PACK),
             )
 
-        offs_t = keep.tile([P, S // 16], U16, name="offs_t")
-        west_t = keep.tile([P, S // 16], U16, name="west_t")
-        east_t = keep.tile([P, S // 16], U16, name="east_t")
-        xs = keep.tile([P, T], U8, name="xs", tag="stage_b", align_bytes=64)
-        zeros = keep.tile([P, H], U8, name="zeros", tag="stage_c", align_bytes=64)
-        w1w_raw = keep.tile([P, 2 * H], U8, name="w1w_raw", tag="stage_a", align_bytes=64)
-        w1s_raw = keep.tile([P, H], U8, name="w1s_raw", tag="stage_d", align_bytes=64)
-        w2w = keep.tile([P, 2 * N], U8, name="w2w", align_bytes=64)
-        gain = keep.tile([P, PACK], F32, name="gain")
-        quarter = keep.tile([P, PACK], F32, name="quarter")
+        def entries(lists, first, width):
+            return lists[:, first // GROUP : (first + width) // GROUP]
 
-        nc.vector.memset(xs[:].bitcast(I32), 0)
-        nc.vector.memset(zeros[:].bitcast(I32), 0)
-        nc.vector.tensor_copy(w1s_raw[:].bitcast(I32), zeros[:].bitcast(I32))
-        xw = keep.tile([P, T], U32, name="xw", tag="stage_c", align_bytes=64)
-
-        nc.sync.dma_start(offs_t[:], offs)
-        nc.gpsimd.dma_start(w1w_raw[:].bitcast(I32), w1_words[0].bitcast(I32))
-        load_scales([nc.sync, nc.sync, nc.scalar, nc.scalar], xs, x_scales)
-        nc.scalar.dma_start(xw[:].bitcast(I32), x_words[0].rearrange("p c r -> p (c r)").bitcast(I32))
-        load_scales([nc.scalar] * 4, w1s_raw, w1_scales)
-        nc.sync.dma_start(west_t[:], west)
-        nc.sync.dma_start(east_t[:], east)
-        nc.gpsimd.dma_start(gain[:], gn.rearrange("(p t) o -> p (t o)", t=PACK))
-        nc.gpsimd.tensor_scalar(quarter[:], gain[:], 0.25, 0.0, ALU.mult, ALU.add)
-        rec_rows = rec.rearrange("(p t) j -> p t j", t=PACK)
-
-        xg_s = keep.tile([P, S], U8, name="xg_s", tag="stage_e", align_bytes=64)
-        nc.vector.tensor_copy(xg_s[:], xs[:].indirect(offs_t[:]))
-        rec0 = keep.tile([P, PACK, HALF], F32, name="rec0", tag="stage_b", align_bytes=64)
-        nc.sync.dma_start(rec0[:], rec_rows[:, :, 0:HALF])
-        w1w = keep.tile([P, 2 * H], U8, name="w1w", align_bytes=64)
-        w1s = keep.tile([P, H], U8, name="w1s", align_bytes=64)
-        deal_words(w1w_raw, w1w)
-        xg_w0 = keep.tile([P, HALF], U32, name="xg_w0", tag="stage_a", align_bytes=64)
-        nc.vector.tensor_copy(xg_w0[:], xw[:].indirect(offs_t[:, 0 : HALF // 16]))
-        deal_scales(w1s_raw, w1s)
-        xg_w1 = keep.tile([P, HALF], U32, name="xg_w1", tag="stage_d", align_bytes=64)
-        nc.vector.tensor_copy(xg_w1[:], xw[:].indirect(offs_t[:, HALF // 16 : S // 16]))
-        xg_w = [xg_w0, xg_w1]
-        w2w_raw = keep.tile([P, 2 * N], U8, name="w2w_raw", tag="stage_c", align_bytes=64)
-        nc.sync.dma_start(w2w_raw[:].bitcast(I32), w2_words[0].bitcast(I32))
-        y = [keep.tile([P, S], F32, name="y%d" % t) for t in range(PACK)]
-        sq = [[keep.tile([P, HALF], F32, name="sq%d_%d" % (t, h)) for h in range(2)] for t in range(PACK)]
-        rg = [[keep.tile([P, HALF], F32, name="rg%d_%d" % (t, h)) for h in range(2)] for t in range(PACK)]
-        cub = [[keep.tile([P, HALF], F32, name="cub%d_%d" % (t, h)) for h in range(2)] for t in range(PACK)]
-        def first_product(acc, t, h):
+        def product(acc, words, scales, t, moving_words, moving_scales):
             nc.tensor.matmul_mx(
                 acc,
-                lhsT=w1w[:, 2 * P * t : 2 * P * (t + 1)].bitcast(FP4X4),
-                lhsT_scale=w1s[:, P * t : P * (t + 1)],
-                rhs=xg_w[h][:].bitcast(FP8X4),
-                rhs_scale=xg_s[:, h * HALF : (h + 1) * HALF],
+                lhsT=words[:, 2 * P * t : 2 * P * (t + 1)].bitcast(FP4X4),
+                lhsT_scale=scales[:, P * t : P * (t + 1)],
+                rhs=moving_words.bitcast(FP8X4),
+                rhs_scale=moving_scales,
                 start=True,
                 stop=True,
             )
 
-        acc0 = [psum.tile([P, HALF], F32, name="acc0_%d" % h, tag="bank%d" % h) for h in range(2)]
-        acc = [None] + [psum.tile([P, S], F32, name="acc%d" % t, tag="bank%d" % (t + 1)) for t in range(1, PACK)]
+        offs_list = keep.tile([P, S // GROUP], U16, name="offs_list")
+        west_lists = keep.tile([P, S // GROUP], U16, name="west_lists")
+        east_lists = keep.tile([P, S // GROUP], U16, name="east_lists")
+        x_scale_table = keep.tile([P, T], U8, name="x_scale_table", tag="stage_b", align_bytes=64)
+        zeros = keep.tile([P, H // 2], U8, name="zeros", tag="stage_c", align_bytes=64)
+        w1_words_raw = keep.tile([P, 2 * H], U8, name="w1_words_raw", tag="stage_a")
+        w1_scales_raw = keep.tile([P, H], U8, name="w1_scales_raw", tag="stage_d", align_bytes=64)
+        w2_words_raw = keep.tile([P, 2 * N], U8, name="w2_words_raw")
+        warm_in = keep.tile([P, 1], F32, name="warm_in")
+        warm_out = keep.tile([P, 1], F32, name="warm_out")
+        gain = keep.tile([P, PACK], F32, name="gain")
+        quarter_gain = keep.tile([P, PACK], F32, name="quarter_gain")
+
+        nc.vector.memset(x_scale_table[:].bitcast(I32), 0)
+        nc.vector.memset(zeros[:].bitcast(I32), 0)
+        nc.vector.tensor_copy(w1_scales_raw[:, 0 : H // 2].bitcast(I32), zeros[:].bitcast(I32))
+        nc.vector.memset(w1_scales_raw[:, H // 2 : H].bitcast(I32), 0)
+        w2_scales_raw = keep.tile([P, N], U8, name="w2_scales_raw")
+        nc.vector.memset(w2_scales_raw[:].bitcast(I32), 0)
+        x_word_table = keep.tile([P, T], U32, name="x_word_table", tag="stage_c", align_bytes=64)
+
+        nc.sync.dma_start(offs_list[:], offs)
+        nc.gpsimd.dma_start(w1_words_raw[:].bitcast(I32), w1_words[0].bitcast(I32))
+        load_scales([nc.sync, nc.sync, nc.scalar, nc.scalar], x_scale_table, x_scales)
+        nc.scalar.dma_start(x_word_table[:].bitcast(I32), x_words[0].rearrange("p c r -> p (c r)").bitcast(I32))
+        load_scales([nc.scalar] * QUADRANTS, w1_scales_raw, w1_scales)
+        load_scales([nc.scalar] * QUADRANTS, w2_scales_raw, w2_scales)
+        nc.sync.dma_start(west_lists[:], west)
+        nc.sync.dma_start(east_lists[:], east)
+        nc.vector.memset(warm_in[:], 0.0)
+        nc.scalar.activation(warm_out[:], warm_in[:], ACT.Tanh)
+        nc.gpsimd.dma_start(w2_words_raw[:].bitcast(I32), w2_words[0].bitcast(I32))
+        nc.gpsimd.dma_start(gain[:], gn.rearrange("(p t) o -> p (t o)", t=PACK))
+        nc.gpsimd.tensor_scalar(quarter_gain[:], gain[:], 0.25, 0.0, ALU.mult, ALU.add)
+        rec_rows = rec.rearrange("(p t) j -> p t j", t=PACK)
+
+        picked_scales = keep.tile([P, S], U8, name="picked_scales", tag="stage_e", align_bytes=64)
+        nc.vector.tensor_copy(picked_scales[:], x_scale_table[:].indirect(offs_list[:]))
+        w1_words_dealt = keep.tile([P, 2 * H], U8, name="w1_words_dealt", tag="stage_b", align_bytes=64)
+        picked_low = keep.tile([P, HALF], U32, name="picked_low", align_bytes=64)
+        nc.vector.tensor_copy(picked_low[:], x_word_table[:].indirect(entries(offs_list, 0, HALF)))
+        deal_words(w1_words_raw, w1_words_dealt[:])
+        rec_first = keep.tile([P, 2, S], F32, name="rec_first", tag="stage_a")
+        nc.sync.dma_start(rec_first[:], rec_rows[:, 0:2, :])
+        w1_scales_dealt = keep.tile([P, H], U8, name="w1_scales_dealt", align_bytes=64)
+        deal_scales(w1_scales_raw, w1_scales_dealt[:])
+        picked_high = keep.tile([P, HALF], U32, name="picked_high", tag="stage_d", align_bytes=64)
+        nc.vector.tensor_copy(picked_high[:], x_word_table[:].indirect(entries(offs_list, HALF, HALF)))
+        picked_words = [picked_low, picked_high]
+        w2_dealt = keep.tile([P, 3 * N], U8, name="w2_dealt", tag="stage_c", align_bytes=64)
+        w2_words_dealt = w2_dealt[:, 0 : 2 * N]
+        w2_scales_dealt = w2_dealt[:, 2 * N : 3 * N]
+        deal_words(w2_words_raw, w2_words_dealt)
+        deal_scales(w2_scales_raw, w2_scales_dealt)
+
+        y = [keep.tile([P, S], F32, name="y%d" % t) for t in range(PACK)]
+        square = [keep.tile([P, S], F32, name="square%d" % t) for t in range(PACK)]
+        gained_rec = [keep.tile([P, S], F32, name="gained_rec%d" % t) for t in range(PACK)]
+        cubic = [keep.tile([P, S], F32, name="cubic%d" % t) for t in range(PACK)]
+
+        first_halves = [psum.tile([P, HALF], F32, name="first_half%d" % h, tag="bank%d" % h) for h in range(2)]
+        first_whole = {t: psum.tile([P, S], F32, name="first_whole%d" % t, tag="bank%d" % (t + 1)) for t in range(1, PACK)}
         for t in range(PACK):
             for h in range(2):
-                first_product(acc0[h][:] if t == 0 else acc[t][:, h * HALF : (h + 1) * HALF], t, h)
-        alpha = math.sqrt(1.25)
-        rec1 = keep.tile([P, PACK, HALF], F32, name="rec1", tag="stage_e", align_bytes=64)
-        nc.sync.dma_start(rec1[:], rec_rows[:, :, HALF:S])
-        rec_t = [rec0, rec1]
-        w2s_raw = keep.tile([P, N], U8, name="w2s_raw", tag="stage_a", align_bytes=64)
-        nc.gpsimd.memset(w2s_raw[:].bitcast(I32), 0)
-        load_scales([nc.sync] * 4, w2s_raw, w2_scales)
-        w2s = keep.tile([P, N], U8, name="w2s", align_bytes=64)
+                cols = slice(h * HALF, (h + 1) * HALF)
+                acc = first_halves[h][:] if t == 0 else first_whole[t][:, cols]
+                product(acc, w1_words_dealt, w1_scales_dealt, t, picked_words[h][:], picked_scales[:, cols])
+        rec_second = keep.tile([P, 2, S], F32, name="rec_second", tag="stage_e", align_bytes=64)
+        nc.sync.dma_start(rec_second[:], rec_rows[:, 2:4, :])
+        rec_pairs = [rec_first, rec_second]
 
-        def square(t, h):
-            nc.scalar.activation(sq[t][h][:], y[t][:, h * HALF : (h + 1) * HALF], ACT.Square, scale=alpha)
+        def potentials(t, cols, acc):
+            nc.scalar.activation(y[t][:, cols], acc, ACT.Tanh)
+            nc.scalar.activation(square[t][:, cols], y[t][:, cols], ACT.Square, scale=math.sqrt(1.25))
 
-        def scale_rec(t, h):
-            nc.scalar.activation(rg[t][h][:], rec_t[h][:, t, :], ACT.Copy, scale=gain[:, t : t + 1])
+        def scale_rec(t):
+            nc.scalar.activation(gained_rec[t][:], rec_pairs[t // 2][:, t % 2, :], ACT.Copy, scale=gain[:, t : t + 1])
 
-        for t in range(PACK):
-            if t == 0:
-                nc.scalar.activation(y[0][:, 0:HALF], acc0[0][:], ACT.Tanh)
-                square(0, 0)
-                nc.scalar.activation(y[0][:, HALF:S], acc0[1][:], ACT.Tanh)
-            else:
-                nc.scalar.activation(y[t][:], acc[t][:], ACT.Tanh)
-                square(t, 0)
-            scale_rec(t, 0)
-        for t in range(PACK):
-            square(t, 1)
-            scale_rec(t, 1)
+        for h in range(2):
+            potentials(0, slice(h * HALF, (h + 1) * HALF), first_halves[h][:])
+        for t in range(1, PACK):
+            potentials(t, slice(0, S), first_whole[t][:])
+            scale_rec(t - 1)
+        scale_rec(PACK - 1)
 
-        ow = keep.tile([P, S], U32, name="ow", align_bytes=64)
-        osc = keep.tile([P, S], U8, name="osc", align_bytes=64)
+        out_word_tile = keep.tile([P, S], U32, name="out_word_tile", align_bytes=64)
+        out_scale_tile = keep.tile([P, S], U8, name="out_scale_tile", align_bytes=64)
         out_rows = out_0.rearrange("(p t) j -> p t j", t=PACK)
         out_words = out_1[0].rearrange("p c r -> p (c r)").bitcast(I32)
 
-        def front(ci):
-            c0, w = CHUNKS[ci]
-            h, o = divmod(c0, HALF)
-            lists = slice(c0 // 16, (c0 + w) // 16)
-            zb = keep.tile([P, PACK, w], BF16, name="zb%d" % ci)
-            g1 = [keep.tile([P, w], F32, name="g1%d_%d" % (ci, t)) for t in range(PACK)]
-            g2 = [keep.tile([P, w], F32, name="g2%d_%d" % (ci, t)) for t in range(PACK)]
+        z_tiles = [keep.tile([P, PACK, w], BF16, name="z_tiles%d" % c) for c, (first, w) in enumerate(CHUNKS)]
+        west_sum = {}
+        both_sum = {}
 
-            def step(k, t):
-                if k == 0:
-                    if o == 0:
-                        nc.vector.scalar_tensor_tensor(cub[t][h][:], sq[t][h][:], 4.0, y[t][:, c0 : c0 + HALF], ALU.subtract, ALU.mult)
-                elif k == 1:
-                    nc.vector.tensor_tensor(g1[t][:], y[t][:].indirect(west_t[:, lists]), cub[t][h][:, o : o + w], ALU.subtract)
-                elif k == 2:
-                    nc.vector.tensor_tensor(g2[t][:], y[t][:].indirect(east_t[:, lists]), g1[t][:], ALU.add)
-                else:
-                    nc.vector.scalar_tensor_tensor(zb[:, t, :], g2[t][:], quarter[:, t : t + 1], rg[t][h][:, o : o + w], ALU.mult, ALU.subtract)
+        def make_cubic(t, h):
+            cols = slice(h * HALF, (h + 1) * HALF)
+            nc.vector.scalar_tensor_tensor(cubic[t][:, cols], square[t][:, cols], 4.0, y[t][:, cols], ALU.subtract, ALU.mult)
 
-            for pair in range(2):
-                for k in range(4):
-                    for t in (2 * pair, 2 * pair + 1):
-                        step(k, t)
-            return zb
+        def add_west(c, t, tag):
+            first, w = CHUNKS[c]
+            west_sum[c, t] = keep.tile([P, w], F32, name="west_sum", tag=tag, align_bytes=64)
+            looked_up = y[t][:].indirect(entries(west_lists, first, w))
+            nc.vector.tensor_tensor(west_sum[c, t][:], looked_up, cubic[t][:, first : first + w], ALU.subtract)
 
-        def back(ci, zb):
-            c0, w = CHUNKS[ci]
-            last = ci == len(CHUNKS) - 1
-            zi = keep.tile([P, w, PACK], BF16, name="zi%d" % ci, align_bytes=64)
-            if last:
-                nc.vector.tensor_copy(zi[:], zb[:].rearrange("p t c -> p c t"))
+        def add_east(c, t, target):
+            first, w = CHUNKS[c]
+            both_sum[c, t] = target
+            looked_up = y[t][:].indirect(entries(east_lists, first, w))
+            nc.vector.tensor_tensor(target, looked_up, west_sum[c, t][:], ALU.add)
+
+        def combine(c, t):
+            first, w = CHUNKS[c]
+            nc.vector.scalar_tensor_tensor(
+                z_tiles[c][:, t, :],
+                both_sum[c, t],
+                quarter_gain[:, t : t + 1],
+                gained_rec[t][:, first : first + w],
+                ALU.mult,
+                ALU.subtract,
+            )
+
+        def second_layer(c):
+            first, w = CHUNKS[c]
+            z_woven = keep.tile([P, w, PACK], BF16, name="z_woven", tag="z_woven%d" % c, align_bytes=64)
+            if c == LAST:
+                nc.vector.tensor_copy(z_woven[:], z_tiles[c][:].rearrange("p t c -> p c t"))
             else:
-                nc.scalar.copy(zi[:], zb[:].rearrange("p t c -> p c t"))
-            zw = keep.tile([P, w], U32, name="zw%d" % ci, align_bytes=64)
-            zs = keep.tile([P, w], U8, name="zs%d" % ci, align_bytes=64)
-            nc.vector.quantize_mx(zw[:].bitcast(FP8X4), zs[:], zi[:].rearrange("p c t -> p (c t)"))
-            per_bank = S // w
-            staged = keep.tile([P, PACK, w], F32, name="staged%d" % ci)
-            banks = []
-            for b in range(PACK // per_bank):
-                bank = psum.tile([P, per_bank, w], F32, name="o%d_%d" % (ci, b), tag="bank%d" % ((5 + 2 * ci + b) % 8))
-                banks.append(bank)
+                nc.scalar.copy(z_woven[:], z_tiles[c][:].rearrange("p t c -> p c t"))
+            z_words = keep.tile([P, w], U32, name="z_words%d" % c, align_bytes=64)
+            z_scales = keep.tile([P, w], U8, name="z_scales%d" % c, align_bytes=64)
+            nc.vector.quantize_mx(z_words[:].bitcast(FP8X4), z_scales[:], z_woven[:].rearrange("p c t -> p (c t)"))
+            per_bank = BANK // w
+            staged = keep.tile([P, PACK, w], F32, name="staged%d" % c)
+            for b, number in enumerate(SECOND_BANKS[c]):
+                bank = psum.tile([P, per_bank, w], F32, name="second", tag="bank%d" % number)
                 for u in range(per_bank):
-                    t = b * per_bank + u
-                    nc.tensor.matmul_mx(
-                        bank[:, u, :],
-                        lhsT=w2w[:, 2 * P * t : 2 * P * (t + 1)].bitcast(FP4X4),
-                        lhsT_scale=w2s[:, P * t : P * (t + 1)],
-                        rhs=zw[:].bitcast(FP8X4),
-                        rhs_scale=zs[:],
-                        start=True,
-                        stop=True,
-                    )
+                    product(bank[:, u, :], w2_words_dealt, w2_scales_dealt, b * per_bank + u, z_words[:], z_scales[:])
                 nc.scalar.copy(staged[:, b * per_bank : (b + 1) * per_bank, :], bank[:])
-            nc.sync.dma_start(out_rows[:, :, c0 : c0 + w], staged[:])
-            oi = keep.tile([P, w, PACK], BF16, name="oi%d" % ci, align_bytes=64)
-            if last:
-                nc.vector.tensor_copy(oi[:], staged[:].rearrange("p t c -> p c t"))
+            nc.sync.dma_start(out_rows[:, :, first : first + w], staged[:])
+            out_woven = keep.tile([P, w, PACK], BF16, name="out_woven%d" % c, align_bytes=64)
+            if c == 0:
+                nc.scalar.copy(out_woven[:], staged[:].rearrange("p t c -> p c t"))
             else:
-                nc.scalar.copy(oi[:], staged[:].rearrange("p t c -> p c t"))
-            return oi
+                nc.vector.tensor_copy(out_woven[:], staged[:].rearrange("p t c -> p c t"))
+            return out_woven
 
-        def finish(ci, oi):
-            c0, w = CHUNKS[ci]
-            nc.vector.quantize_mx(ow[:, c0 : c0 + w].bitcast(FP8X4), osc[:, c0 : c0 + w], oi[:].rearrange("p c t -> p (c t)"))
-            nc.sync.dma_start(out_words[:, c0 : c0 + w], ow[:, c0 : c0 + w].bitcast(I32))
+        for t in range(PACK):
+            for h in range(2):
+                make_cubic(t, h)
+            for c in range(LAST):
+                add_west(c, t, "west%d_%d" % (c, t))
+            for c in range(LAST):
+                first, w = CHUNKS[c]
+                add_east(c, t, keep.tile([P, w], F32, name="both_sum", tag="both%d_%d" % (c, t), align_bytes=64)[:])
+            for c in range(LAST):
+                combine(c, t)
+        woven = [second_layer(c) for c in range(LAST)]
 
-        oi = []
-        for ci in range(len(CHUNKS)):
-            zb = front(ci)
-            if ci == 0:
-                deal_words(w2w_raw, w2w)
-                deal_scales(w2s_raw, w2s)
-            oi.append(back(ci, zb))
-        for ci in range(len(CHUNKS)):
-            finish(ci, oi[ci])
-        for q in range(4):
+        for t in range(PACK):
+            add_west(LAST, t, "%s%d_%d" % ("west" if t < 2 else "both", t % 2, PACK - 1))
+        for c in range(LAST):
+            pair = keep.tile([P, 2, CHUNKS[LAST][1]], F32, name="pair", tag="z_woven%d" % c, align_bytes=64)
+            for u in range(2):
+                add_east(LAST, 2 * c + u, pair[:, u, :])
+        for t in range(PACK):
+            combine(LAST, t)
+        woven.append(second_layer(LAST))
+
+        for (first, w), out_woven in zip(CHUNKS, woven):
+            cols = slice(first, first + w)
+            nc.vector.quantize_mx(
+                out_word_tile[:, cols].bitcast(FP8X4), out_scale_tile[:, cols], out_woven[:].rearrange("p c t -> p (c t)")
+            )
+            nc.sync.dma_start(out_words[:, cols], out_word_tile[:, cols].bitcast(I32))
+        for q in range(QUADRANTS):
             queue = nc.scalar if q % 2 else nc.sync
-            queue.dma_start(out_2[0, 4 * q : 4 * q + 4, :].bitcast(I32), osc[32 * q : 32 * q + 4, :].bitcast(I32))
+            queue.dma_start(
+                out_2[0, 4 * q : 4 * q + 4, :].bitcast(I32), out_scale_tile[32 * q : 32 * q + 4, :].bitcast(I32)
+            )

@@ -21,11 +21,11 @@ P = 128
 PACK = 4
 GROUP = 16
 QUADRANTS = 4
-BANK = 512
+RUN = 4
 HALF = S // 2
 CHUNKS = [(0, 256), (256, 128), (384, 128)]
 LAST = len(CHUNKS) - 1
-SECOND_BANKS = [(5, 6), (7,), (1,)]
+SECOND_BANKS = [(5, 6), (7,), (0, 1)]
 
 
 def tile_picked_fhn8_none_po_kernel(
@@ -51,6 +51,9 @@ def tile_picked_fhn8_none_po_kernel(
                 dealt.rearrange("p (t m) -> p t m", t=PACK),
                 raw[:].rearrange("p (m t) -> p t m", t=PACK),
             )
+
+        def weave(move, target, tiles):
+            move(target[:].rearrange("p (c i) t -> p c t i", i=RUN), tiles[:].rearrange("p t (c i) -> p c t i", i=RUN))
 
         def entries(lists, first, width):
             return lists[:, first // GROUP : (first + width) // GROUP]
@@ -190,14 +193,11 @@ def tile_picked_fhn8_none_po_kernel(
         def second_layer(c):
             first, w = CHUNKS[c]
             z_woven = keep.tile([P, w, PACK], BF16, name="z_woven", tag="z_woven%d" % c, align_bytes=64)
-            if c == LAST:
-                nc.vector.tensor_copy(z_woven[:], z_tiles[c][:].rearrange("p t c -> p c t"))
-            else:
-                nc.scalar.copy(z_woven[:], z_tiles[c][:].rearrange("p t c -> p c t"))
+            weave(nc.vector.tensor_copy if c == LAST else nc.scalar.copy, z_woven, z_tiles[c])
             z_words = keep.tile([P, w], U32, name="z_words%d" % c, align_bytes=64)
             z_scales = keep.tile([P, w], U8, name="z_scales%d" % c, align_bytes=64)
             nc.vector.quantize_mx(z_words[:].bitcast(FP8X4), z_scales[:], z_woven[:].rearrange("p c t -> p (c t)"))
-            per_bank = BANK // w
+            per_bank = PACK // len(SECOND_BANKS[c])
             staged = keep.tile([P, PACK, w], F32, name="staged%d" % c)
             for b, number in enumerate(SECOND_BANKS[c]):
                 bank = psum.tile([P, per_bank, w], F32, name="second", tag="bank%d" % number)
@@ -206,10 +206,7 @@ def tile_picked_fhn8_none_po_kernel(
                 nc.scalar.copy(staged[:, b * per_bank : (b + 1) * per_bank, :], bank[:])
             nc.sync.dma_start(out_rows[:, :, first : first + w], staged[:])
             out_woven = keep.tile([P, w, PACK], BF16, name="out_woven%d" % c, align_bytes=64)
-            if c == 0:
-                nc.scalar.copy(out_woven[:], staged[:].rearrange("p t c -> p c t"))
-            else:
-                nc.vector.tensor_copy(out_woven[:], staged[:].rearrange("p t c -> p c t"))
+            weave(nc.scalar.copy if c == 0 else nc.vector.tensor_copy, out_woven, staged)
             return out_woven
 
         for t in range(PACK):

import math
from contextlib import ExitStack

import concourse.mybir as mybir

K, T, S, N, H = 512, 2048, 512, 512, 512
FLOPS = 2 * K * H * S + 2 * H * N * S

F32 = mybir.dt.float32
BF16 = mybir.dt.bfloat16
I32 = mybir.dt.int32
U32 = mybir.dt.uint32
U16 = mybir.dt.uint16
U8 = mybir.dt.uint8
FP8X4 = mybir.dt.float8_e4m3fn_x4
FP4X4 = mybir.dt.float4_e2m1fn_x4
ACT = mybir.ActivationFunctionType
ALU = mybir.AluOpType

P = 128
PACK = 4
GROUP = 16
QUADRANTS = 4
RUN = 4
HALF = S // 2
CHUNKS = [(0, 256), (256, 128), (384, 128)]
LAST = len(CHUNKS) - 1
SECOND_BANKS = [(5, 6), (7,), (0, 1)]


def tile_picked_fhn8_none_po_kernel(
    tc, x_words, x_scales, w1_words, w1_scales, rec, gn, w2_words, w2_scales, offs, west, east, out_0, out_1, out_2
):
    nc = tc.nc
    with ExitStack() as ctx:
        keep = ctx.enter_context(tc.tile_pool(name="keep", bufs=1))
        psum = ctx.enter_context(tc.psum_pool(name="psum", bufs=1))

        def load_scales(queues, tile, rows):
            for q, queue in enumerate(queues):
                queue.dma_start(tile[32 * q : 32 * q + 4, :].bitcast(I32), rows[0, 4 * q : 4 * q + 4, :].bitcast(I32))

        def deal_words(raw, dealt):
            nc.vector.tensor_copy(
                dealt.bitcast(U16).rearrange("p (t m) -> p t m", t=PACK),
                raw[:].bitcast(U16).rearrange("p (m t) -> p t m", t=PACK),
            )

        def deal_scales(raw, dealt):
            nc.vector.tensor_copy(
                dealt.rearrange("p (t m) -> p t m", t=PACK),
                raw[:].rearrange("p (m t) -> p t m", t=PACK),
            )

        def weave(move, target, tiles):
            move(target[:].rearrange("p (c i) t -> p c t i", i=RUN), tiles[:].rearrange("p t (c i) -> p c t i", i=RUN))

        def entries(lists, first, width):
            return lists[:, first // GROUP : (first + width) // GROUP]

        def product(acc, words, scales, t, moving_words, moving_scales):
            nc.tensor.matmul_mx(
                acc,
                lhsT=words[:, 2 * P * t : 2 * P * (t + 1)].bitcast(FP4X4),
                lhsT_scale=scales[:, P * t : P * (t + 1)],
                rhs=moving_words.bitcast(FP8X4),
                rhs_scale=moving_scales,
                start=True,
                stop=True,
            )

        offs_list = keep.tile([P, S // GROUP], U16, name="offs_list")
        west_lists = keep.tile([P, S // GROUP], U16, name="west_lists")
        east_lists = keep.tile([P, S // GROUP], U16, name="east_lists")
        x_scale_table = keep.tile([P, T], U8, name="x_scale_table", tag="stage_b", align_bytes=64)
        zeros = keep.tile([P, H // 2], U8, name="zeros", tag="stage_c", align_bytes=64)
        w1_words_raw = keep.tile([P, 2 * H], U8, name="w1_words_raw", tag="stage_a")
        w1_scales_raw = keep.tile([P, H], U8, name="w1_scales_raw", tag="stage_d", align_bytes=64)
        w2_words_raw = keep.tile([P, 2 * N], U8, name="w2_words_raw")
        warm_in = keep.tile([P, 1], F32, name="warm_in")
        warm_out = keep.tile([P, 1], F32, name="warm_out")
        gain = keep.tile([P, PACK], F32, name="gain")
        quarter_gain = keep.tile([P, PACK], F32, name="quarter_gain")

        nc.vector.memset(x_scale_table[:].bitcast(I32), 0)
        nc.vector.memset(zeros[:].bitcast(I32), 0)
        nc.vector.tensor_copy(w1_scales_raw[:, 0 : H // 2].bitcast(I32), zeros[:].bitcast(I32))
        nc.vector.memset(w1_scales_raw[:, H // 2 : H].bitcast(I32), 0)
        w2_scales_raw = keep.tile([P, N], U8, name="w2_scales_raw")
        nc.vector.memset(w2_scales_raw[:].bitcast(I32), 0)
        x_word_table = keep.tile([P, T], U32, name="x_word_table", tag="stage_c", align_bytes=64)

        nc.sync.dma_start(offs_list[:], offs)
        nc.gpsimd.dma_start(w1_words_raw[:].bitcast(I32), w1_words[0].bitcast(I32))
        load_scales([nc.sync, nc.sync, nc.scalar, nc.scalar], x_scale_table, x_scales)
        nc.scalar.dma_start(x_word_table[:].bitcast(I32), x_words[0].rearrange("p c r -> p (c r)").bitcast(I32))
        load_scales([nc.scalar] * QUADRANTS, w1_scales_raw, w1_scales)
        load_scales([nc.scalar] * QUADRANTS, w2_scales_raw, w2_scales)
        nc.sync.dma_start(west_lists[:], west)
        nc.sync.dma_start(east_lists[:], east)
        nc.vector.memset(warm_in[:], 0.0)
        nc.scalar.activation(warm_out[:], warm_in[:], ACT.Tanh)
        nc.gpsimd.dma_start(w2_words_raw[:].bitcast(I32), w2_words[0].bitcast(I32))
        nc.gpsimd.dma_start(gain[:], gn.rearrange("(p t) o -> p (t o)", t=PACK))
        nc.gpsimd.tensor_scalar(quarter_gain[:], gain[:], 0.25, 0.0, ALU.mult, ALU.add)
        rec_rows = rec.rearrange("(p t) j -> p t j", t=PACK)

        picked_scales = keep.tile([P, S], U8, name="picked_scales", tag="stage_e", align_bytes=64)
        nc.vector.tensor_copy(picked_scales[:], x_scale_table[:].indirect(offs_list[:]))
        w1_words_dealt = keep.tile([P, 2 * H], U8, name="w1_words_dealt", tag="stage_b", align_bytes=64)
        picked_low = keep.tile([P, HALF], U32, name="picked_low", align_bytes=64)
        nc.vector.tensor_copy(picked_low[:], x_word_table[:].indirect(entries(offs_list, 0, HALF)))
        deal_words(w1_words_raw, w1_words_dealt[:])
        rec_first = keep.tile([P, 2, S], F32, name="rec_first", tag="stage_a")
        nc.sync.dma_start(rec_first[:], rec_rows[:, 0:2, :])
        w1_scales_dealt = keep.tile([P, H], U8, name="w1_scales_dealt", align_bytes=64)
        deal_scales(w1_scales_raw, w1_scales_dealt[:])
        picked_high = keep.tile([P, HALF], U32, name="picked_high", tag="stage_d", align_bytes=64)
        nc.vector.tensor_copy(picked_high[:], x_word_table[:].indirect(entries(offs_list, HALF, HALF)))
        picked_words = [picked_low, picked_high]
        w2_dealt = keep.tile([P, 3 * N], U8, name="w2_dealt", tag="stage_c", align_bytes=64)
        w2_words_dealt = w2_dealt[:, 0 : 2 * N]
        w2_scales_dealt = w2_dealt[:, 2 * N : 3 * N]
        deal_words(w2_words_raw, w2_words_dealt)
        deal_scales(w2_scales_raw, w2_scales_dealt)

        y = [keep.tile([P, S], F32, name="y%d" % t) for t in range(PACK)]
        square = [keep.tile([P, S], F32, name="square%d" % t) for t in range(PACK)]
        gained_rec = [keep.tile([P, S], F32, name="gained_rec%d" % t) for t in range(PACK)]
        cubic = [keep.tile([P, S], F32, name="cubic%d" % t) for t in range(PACK)]

        first_halves = [psum.tile([P, HALF], F32, name="first_half%d" % h, tag="bank%d" % h) for h in range(2)]
        first_whole = {t: psum.tile([P, S], F32, name="first_whole%d" % t, tag="bank%d" % (t + 1)) for t in range(1, PACK)}
        for t in range(PACK):
            for h in range(2):
                cols = slice(h * HALF, (h + 1) * HALF)
                acc = first_halves[h][:] if t == 0 else first_whole[t][:, cols]
                product(acc, w1_words_dealt, w1_scales_dealt, t, picked_words[h][:], picked_scales[:, cols])
        rec_second = keep.tile([P, 2, S], F32, name="rec_second", tag="stage_e", align_bytes=64)
        nc.sync.dma_start(rec_second[:], rec_rows[:, 2:4, :])
        rec_pairs = [rec_first, rec_second]

        def potentials(t, cols, acc):
            nc.scalar.activation(y[t][:, cols], acc, ACT.Tanh)
            nc.scalar.activation(square[t][:, cols], y[t][:, cols], ACT.Square, scale=math.sqrt(1.25))

        def scale_rec(t):
            nc.scalar.activation(gained_rec[t][:], rec_pairs[t // 2][:, t % 2, :], ACT.Copy, scale=gain[:, t : t + 1])

        for h in range(2):
            potentials(0, slice(h * HALF, (h + 1) * HALF), first_halves[h][:])
        for t in range(1, PACK):
            potentials(t, slice(0, S), first_whole[t][:])
            scale_rec(t - 1)
        scale_rec(PACK - 1)

        out_word_tile = keep.tile([P, S], U32, name="out_word_tile", align_bytes=64)
        out_scale_tile = keep.tile([P, S], U8, name="out_scale_tile", align_bytes=64)
        out_rows = out_0.rearrange("(p t) j -> p t j", t=PACK)
        out_words = out_1[0].rearrange("p c r -> p (c r)").bitcast(I32)

        z_tiles = [keep.tile([P, PACK, w], BF16, name="z_tiles%d" % c) for c, (first, w) in enumerate(CHUNKS)]
        west_sum = {}
        both_sum = {}

        def make_cubic(t, h):
            cols = slice(h * HALF, (h + 1) * HALF)
            nc.vector.scalar_tensor_tensor(cubic[t][:, cols], square[t][:, cols], 4.0, y[t][:, cols], ALU.subtract, ALU.mult)

        def add_west(c, t, tag):
            first, w = CHUNKS[c]
            west_sum[c, t] = keep.tile([P, w], F32, name="west_sum", tag=tag, align_bytes=64)
            looked_up = y[t][:].indirect(entries(west_lists, first, w))
            nc.vector.tensor_tensor(west_sum[c, t][:], looked_up, cubic[t][:, first : first + w], ALU.subtract)

        def add_east(c, t, target):
            first, w = CHUNKS[c]
            both_sum[c, t] = target
            looked_up = y[t][:].indirect(entries(east_lists, first, w))
            nc.vector.tensor_tensor(target, looked_up, west_sum[c, t][:], ALU.add)

        def combine(c, t):
            first, w = CHUNKS[c]
            nc.vector.scalar_tensor_tensor(
                z_tiles[c][:, t, :],
                both_sum[c, t],
                quarter_gain[:, t : t + 1],
                gained_rec[t][:, first : first + w],
                ALU.mult,
                ALU.subtract,
            )

        def second_layer(c):
            first, w = CHUNKS[c]
            z_woven = keep.tile([P, w, PACK], BF16, name="z_woven", tag="z_woven%d" % c, align_bytes=64)
            weave(nc.vector.tensor_copy if c == LAST else nc.scalar.copy, z_woven, z_tiles[c])
            z_words = keep.tile([P, w], U32, name="z_words%d" % c, align_bytes=64)
            z_scales = keep.tile([P, w], U8, name="z_scales%d" % c, align_bytes=64)
            nc.vector.quantize_mx(z_words[:].bitcast(FP8X4), z_scales[:], z_woven[:].rearrange("p c t -> p (c t)"))
            per_bank = PACK // len(SECOND_BANKS[c])
            staged = keep.tile([P, PACK, w], F32, name="staged%d" % c)
            for b, number in enumerate(SECOND_BANKS[c]):
                bank = psum.tile([P, per_bank, w], F32, name="second", tag="bank%d" % number)
                for u in range(per_bank):
                    product(bank[:, u, :], w2_words_dealt, w2_scales_dealt, b * per_bank + u, z_words[:], z_scales[:])
                nc.scalar.copy(staged[:, b * per_bank : (b + 1) * per_bank, :], bank[:])
            nc.sync.dma_start(out_rows[:, :, first : first + w], staged[:])
            out_woven = keep.tile([P, w, PACK], BF16, name="out_woven%d" % c, align_bytes=64)
            weave(nc.scalar.copy if c == 0 else nc.vector.tensor_copy, out_woven, staged)
            return out_woven

        for t in range(PACK):
            for h in range(2):
                make_cubic(t, h)
            for c in range(LAST):
                add_west(c, t, "west%d_%d" % (c, t))
            for c in range(LAST):
                first, w = CHUNKS[c]
                add_east(c, t, keep.tile([P, w], F32, name="both_sum", tag="both%d_%d" % (c, t), align_bytes=64)[:])
            for c in range(LAST):
                combine(c, t)
        woven = [second_layer(c) for c in range(LAST)]

        for t in range(PACK):
            add_west(LAST, t, "%s%d_%d" % ("west" if t < 2 else "both", t % 2, PACK - 1))
        for c in range(LAST):
            pair = keep.tile([P, 2, CHUNKS[LAST][1]], F32, name="pair", tag="z_woven%d" % c, align_bytes=64)
            for u in range(2):
                add_east(LAST, 2 * c + u, pair[:, u, :])
        for t in range(PACK):
            combine(LAST, t)
        woven.append(second_layer(LAST))

        for (first, w), out_woven in zip(CHUNKS, woven):
            cols = slice(first, first + w)
            nc.vector.quantize_mx(
                out_word_tile[:, cols].bitcast(FP8X4), out_scale_tile[:, cols], out_woven[:].rearrange("p c t -> p (c t)")
            )
            nc.sync.dma_start(out_words[:, cols], out_word_tile[:, cols].bitcast(I32))
        for q in range(QUADRANTS):
            queue = nc.scalar if q % 2 else nc.sync
            queue.dma_start(
                out_2[0, 4 * q : 4 * q + 4, :].bitcast(I32), out_scale_tile[32 * q : 32 * q + 4, :].bitcast(I32)
            )
